import numpy as np
import ml_dtypes


def mxq(x, axis, fmt="e4m3"):
    dtype, down = {"e4m3": (ml_dtypes.float8_e4m3fn, 7), "e5m2": (ml_dtypes.float8_e5m2, 14)}[fmt]
    v = np.moveaxis(np.asarray(x, np.float32).astype(ml_dtypes.bfloat16).astype(np.float64), axis, -1)
    blocks = v.reshape(v.shape[:-1] + (-1, 32))
    amax = np.abs(blocks).max(-1, keepdims=True)
    byte = np.maximum(np.where(amax > 0, np.frexp(amax)[1] - 1 + 127, 0) - down, 1)
    scale = np.exp2(byte - 127.0)
    codes = (blocks / scale).astype(np.float32).astype(dtype).astype(np.float64)
    return np.moveaxis((codes * scale).reshape(v.shape), -1, axis)


WIDE = False


def mx_kscale(k):
    if not WIDE:
        return np.ones(k)
    levels = np.array([10, -10, 5, -5, 0])
    if k % 512:
        return np.exp2(np.random.permutation(np.resize(levels, k // 32))).repeat(32)
    a = np.empty((k // 512, 16))
    for p in range(k // 512):
        a[p, :8] = np.random.permutation(np.resize(levels, 8))
        for g in range(8):
            far = levels[np.abs(levels - a[p, g]) >= 10]
            a[p, g + 8] = far[np.random.randint(len(far))]
    return np.exp2(a.ravel()).repeat(32)


def f64(x):
    return np.asarray(x).astype(np.float64)


def striped(idx):
    return np.tile(np.asarray(idx).reshape(-1, 16).T, (8, 1)).astype(np.uint16)


def unstriped(offs):
    return offs[:16].T.reshape(-1).astype(np.int64)


E2M1 = np.array([0.0, 0.5, 1.0, 1.5, 2.0, 3.0, 4.0, 6.0, -0.0, -0.5, -1.0, -1.5, -2.0, -3.0, -4.0, -6.0])


def pack_weight(w, fmt):
    k, n = w.shape
    w = f64(np.asarray(w, np.float32).astype(ml_dtypes.bfloat16)).reshape(k // 32, 32, n)
    amax = np.abs(w).max(1)
    if fmt == "e4m3":
        byte = np.frexp(amax)[1] - 1 + 127 - 7
    else:
        mant, ex = np.frexp(amax / 6.0)
        byte = np.where(mant > 0.5, ex, ex - 1) + 127
    byte = np.clip(np.where(amax > 0, byte, 1), 1, 254)
    scaled = (w * np.exp2(127.0 - byte)[:, None, :]).reshape(k, n).astype(np.float32)
    by_word = np.ascontiguousarray(scaled.reshape(k // 512, 128, 4, n).transpose(0, 1, 3, 2))
    if fmt == "e4m3":
        words = by_word.astype(ml_dtypes.float8_e4m3fn).view(np.uint8)
    else:
        c = by_word.astype(ml_dtypes.float4_e2m1fn).view(np.uint8) & 0xF
        words = (c[..., 0::2] | (c[..., 1::2] << 4)).reshape(k // 512, 128, 2 * n)
    return np.ascontiguousarray(words), np.ascontiguousarray(byte.astype(np.uint8).reshape(k // 512, 16, n))


def unpack_weight(words, scales, fmt):
    g, _, n = scales.shape
    words = np.ascontiguousarray(words).reshape(g, 128, n, -1)
    if fmt == "e4m3":
        vals = words.view(ml_dtypes.float8_e4m3fn).astype(np.float64)
    else:
        nib = np.empty((g, 128, n, 4), np.uint8)
        nib[..., 0::2] = words & 0xF
        nib[..., 1::2] = words >> 4
        vals = E2M1[nib]
    vals = vals * np.repeat(np.exp2(scales.astype(np.float64) - 127.0), 8, axis=1)[..., None]
    return vals.transpose(0, 1, 3, 2).reshape(g * 512, n)


D, T, I, Q, E, Z, M = 512, 2048, 512, 512, 512, 1024, 1024


def setup_inputs():
    n = np.random.standard_normal
    idx = np.random.permutation(T)[:I]
    idx2 = np.random.permutation(Z)[:I]
    idx3 = np.random.permutation(M)[:I]
    fd = mx_kscale(D)
    fq = mx_kscale(Q)
    keysp = pack_weight(n((D, T)) / fd[:, None], "e4m3")
    return {
        "query": (n((D, Q)) * 1.0 / np.sqrt(D) * fd[:, None]).astype(np.float32),
        "keys_words": keysp[0],
        "keys_scales": keysp[1],
        "earl": (np.random.uniform(0.3, 1.7, (Q, Z))).astype(np.float32),
        "qs": (np.random.uniform(0.5, 2.0, (Q, 1)) * fq[:, None]).astype(np.float32),
        "msgs": (n((Q, E)) * 1 / np.sqrt(Q) / fq[:, None]).astype(np.float32),
        "old": (n((E, M)) * 1.0).astype(np.float32),
        "offs": striped(idx),
        "offs2": striped(idx2),
        "offs3": striped(idx3),
    }


def reference(query, keys_words, keys_scales, earl, qs, msgs, old, offs, offs2, offs3):
    idx = unstriped(offs)
    idx2 = unstriped(offs2)
    idx3 = unstriped(offs3)
    keysu = unpack_weight(keys_words, keys_scales, "e4m3")
    queryq = mxq(f64(query), 0, "e4m3")
    keysidxg = keysu[:, idx]
    a = queryq.T @ keysidxg
    w = a * f64(earl)[:, idx2]
    wq = w * f64(qs)
    msgsq = mxq(f64(msgs), 0, "e4m3")
    wqq = mxq(wq, 0, "e4m3")
    dl = msgsq.T @ wqq
    df = np.zeros((E, M))
    df[:, idx3] = dl
    y = f64(old) + df
    return y

@@ -1,0 +1,235 @@
+from contextlib import ExitStack
+
+import concourse.mybir as mybir
+
+F32 = mybir.dt.float32
+BF16 = mybir.dt.bfloat16
+I32 = mybir.dt.int32
+U32 = mybir.dt.uint32
+U16 = mybir.dt.uint16
+U8 = mybir.dt.uint8
+FP8X4 = mybir.dt.float8_e4m3fn_x4
+MULT = mybir.AluOpType.mult
+ADD = mybir.AluOpType.add
+COPY = mybir.ActivationFunctionType.Copy
+
+D, T, I, Q, E, Z, M = 512, 2048, 512, 512, 512, 1024, 1024
+P = 128
+PACK = 4
+HALF = I // 2
+LIST_COLS = I // 16
+SPLIT = 384
+FLOPS = 2 * D * Q * I + 2 * Q * E * I
+
+
+def tile_attend_earliertable_deliveredplanes_lean_kernel(
+    tc, query, keys_words, keys_scales, earl, qs, msgs, old, offs, offs2, offs3, out
+):
+    nc = tc.nc
+    with ExitStack() as ctx:
+        lists = ctx.enter_context(tc.tile_pool(name="lists", bufs=1))
+        sb = ctx.enter_context(tc.tile_pool(name="sb", bufs=1))
+        psum = ctx.enter_context(tc.psum_pool(name="psum", bufs=1))
+
+        def slots(h):
+            return slice(h * HALF, (h + 1) * HALF)
+
+        key_list = lists.tile([P, LIST_COLS], U16, name="key_list")
+        earl_list = lists.tile([P, LIST_COLS], U16, name="earl_list")
+        place_list = lists.tile([P, LIST_COLS], U16, name="place_list")
+
+        pool_scales = sb.tile([P, T], U8, name="pool_scales", align_bytes=64)
+        pool_words = sb.tile([P, T], I32, name="pool_words", align_bytes=64)
+        query_raw = sb.tile([P, PACK, Q], F32, name="query_raw")
+        earl_rows = [sb.tile([P, Z], F32, name=f"earl_rows{r}") for r in range(PACK)]
+        row_factor = sb.tile([P, PACK], F32, name="row_factor")
+        msgs_raw = [sb.tile([P, PACK, 2 * P], F32, name=f"msgs_raw{u}", tag=f"msgs_raw{u}") for u in range(2)]
+        old_rows = [sb.tile([P, M], F32, name=f"old_rows{k}") for k in range(E // P)]
+        placed = [sb.tile([P, M], F32, name=f"placed{k}") for k in range(E // P)]
+
+        nc.vector.memset(pool_scales[:].bitcast(I32), 0)
+        for k in range(E // P):
+            nc.vector.memset(placed[k][:], 0.0)
+
+        nc.sync.dma_start(key_list[:], offs)
+        nc.sync.dma_start(out=query_raw[:], in_=query.rearrange("(p j) q -> p j q", j=PACK))
+        for quad in range(4):
+            nc.sync.dma_start(
+                out=pool_scales[32 * quad : 32 * quad + 4, :].bitcast(I32),
+                in_=keys_scales[0, 4 * quad : 4 * quad + 4, :].bitcast(I32),
+            )
+        nc.sync.dma_start(
+            out=pool_words[:], in_=keys_words[0].rearrange("p n t -> p (n t)").bitcast(I32)
+        )
+        earl_by_place = earl.rearrange("(p r) z -> r p z", r=PACK)
+        nc.sync.dma_start(out=earl_rows[0][:], in_=earl_by_place[0])
+        nc.sync.dma_start(earl_list[:], offs2)
+        nc.sync.dma_start(out=row_factor[:], in_=qs.rearrange("(p r) o -> p (r o)", r=PACK))
+        nc.sync.dma_start(place_list[:], offs3)
+        for r in range(1, PACK):
+            nc.sync.dma_start(out=earl_rows[r][:], in_=earl_by_place[r])
+        msgs_by_word = msgs.rearrange("(p j) e -> p j e", j=PACK)
+        for u in range(2):
+            nc.sync.dma_start(out=msgs_raw[u][:], in_=msgs_by_word[:, :, u * 2 * P : (u + 1) * 2 * P])
+        for k in range(E // P):
+            nc.sync.dma_start(out=old_rows[k][:], in_=old[k * P : (k + 1) * P, :])
+
+        query_bf = sb.tile([P, PACK, P, PACK], BF16, name="query_bf", align_bytes=64)
+        nc.scalar.copy(
+            out=query_bf[:].rearrange("p r s j -> p s j r"),
+            in_=query_raw[:].rearrange("p j (s r) -> p s j r", r=PACK),
+        )
+        key_scales = sb.tile([P, I], U8, name="key_scales", align_bytes=64)
+        key_words = sb.tile([P, I], U32, name="key_words", align_bytes=64)
+        nc.vector.tensor_copy(key_scales[:], pool_scales[:].indirect(key_list[:]))
+        query_codes = sb.tile([P, Q], U32, name="query_codes", align_bytes=64)
+        query_scales = sb.tile([P, Q], U8, name="query_scales", align_bytes=64)
+        nc.vector.quantize_mx(
+            out=query_codes[:].bitcast(FP8X4),
+            scales=query_scales[:],
+            in_=query_bf[:].rearrange("p r s j -> p (r s j)"),
+        )
+        nc.vector.tensor_copy(key_words[:], pool_words[:].bitcast(U32).indirect(key_list[:]))
+
+        scores = [psum.tile([P, I], F32, name=f"scores{r}", tag=f"bank{r}") for r in range(PACK)]
+        for r in range(PACK):
+            cols = slice(r * P, (r + 1) * P)
+            nc.tensor.matmul_mx(
+                out=scores[r][:],
+                lhsT=query_codes[:, cols].bitcast(FP8X4),
+                lhsT_scale=query_scales[:, cols],
+                rhs=key_words[:].bitcast(FP8X4),
+                rhs_scale=key_scales[:],
+                start=True,
+                stop=True,
+            )
+
+        earl_listed = [sb.tile([P, I], F32, name=f"earl_listed{r}") for r in range(PACK)]
+        weights = sb.tile([P, 2, PACK, HALF], BF16, name="weights")
+
+        def look_up(engine, r, h0, h1):
+            window = earl_rows[r][:].indirect(earl_list[:, h0 * HALF // 16 : h1 * HALF // 16])
+            if engine is nc.scalar:
+                nc.scalar.activation(earl_listed[r][:, h0 * HALF : h1 * HALF], window, COPY)
+            else:
+                nc.vector.tensor_copy(earl_listed[r][:, h0 * HALF : h1 * HALF], window)
+
+        def weigh(r, h0, h1):
+            nc.vector.scalar_tensor_tensor(
+                out=weights[:, h0:h1, r, :],
+                in0=scores[r][:].rearrange("p (h i) -> p h i", h=2)[:, h0:h1, :],
+                scalar=row_factor[:, r : r + 1],
+                in1=earl_listed[r][:].rearrange("p (h i) -> p h i", h=2)[:, h0:h1, :],
+                op0=MULT,
+                op1=MULT,
+            )
+
+        w_bf = {}
+        w_codes = sb.tile([P, I], U32, name="w_codes", align_bytes=64)
+        w_scales = sb.tile([P, I], U8, name="w_scales", align_bytes=64)
+
+        def weave(h):
+            w_bf[h] = sb.tile([P, HALF, PACK], BF16, name=f"w_bf{h}", tag="w_bf", align_bytes=64)
+            nc.vector.tensor_copy(
+                out=w_bf[h][:].rearrange("p (c i) r -> p c r i", i=4),
+                in_=weights[:, h, :, :].rearrange("p r (c i) -> p c r i", i=4),
+            )
+
+        def quantise_w(h):
+            nc.vector.quantize_mx(
+                out=w_codes[:, slots(h)].bitcast(FP8X4),
+                scales=w_scales[:, slots(h)],
+                in_=w_bf[h][:].rearrange("p i r -> p (i r)"),
+            )
+
+        m_bf = [sb.tile([P, 2 * P, PACK], BF16, name=f"m_bf{u}", align_bytes=64) for u in range(2)]
+        m_codes = [sb.tile([P, 2 * P], U32, name=f"m_codes{u}", align_bytes=64) for u in range(2)]
+        m_scales = [sb.tile([P, 2 * P], U8, name=f"m_scales{u}", align_bytes=64) for u in range(2)]
+
+        def round_msgs(u):
+            nc.scalar.copy(
+                out=m_bf[u][:].rearrange("p (c i) j -> p c j i", i=4),
+                in_=msgs_raw[u][:].rearrange("p j (c i) -> p c j i", i=4),
+            )
+
+        def quantise_m(u):
+            nc.vector.quantize_mx(
+                out=m_codes[u][:].bitcast(FP8X4),
+                scales=m_scales[u][:],
+                in_=m_bf[u][:].rearrange("p e j -> p (e j)"),
+            )
+
+        def product(dst, k, cols):
+            mcols = slice((k % 2) * P, (k % 2 + 1) * P)
+            nc.tensor.matmul_mx(
+                out=dst,
+                lhsT=m_codes[k // 2][:, mcols].bitcast(FP8X4),
+                lhsT_scale=m_scales[k // 2][:, mcols],
+                rhs=w_codes[:, cols].bitcast(FP8X4),
+                rhs_scale=w_scales[:, cols],
+                start=True,
+                stop=True,
+            )
+
+        def deliver_pair(h, tag):
+            bank = psum.tile([P, 2, HALF], F32, name=f"pair_bank{h}")
+            for k in range(2):
+                product(bank[:, k, :], k, slots(h))
+            sums = sb.tile([P, 2, HALF], F32, name=f"pair_sums{h}", tag=tag)
+            nc.scalar.copy(out=sums[:], in_=bank[:])
+            return sums
+
+        def deliver_whole(k):
+            bank = psum.tile([P, I], F32, name=f"whole_bank{k}")
+            product(bank[:], k, slice(0, I))
+            sums = sb.tile([P, I], F32, name=f"whole_sums{k}")
+            nc.scalar.copy(out=sums[:], in_=bank[:])
+            return sums
+
+        def place(engine, k, values, lo, hi):
+            window = placed[k][:].indirect(place_list[:, lo // 16 : hi // 16])
+            if engine is nc.scalar:
+                nc.scalar.activation(window, values, COPY)
+            else:
+                nc.vector.tensor_copy(window, values)
+
+        def finish(engine, k, parts):
+            for c in range(parts):
+                cols = slice(c * (M // parts), (c + 1) * (M // parts))
+                engine.tensor_tensor(old_rows[k][:, cols], old_rows[k][:, cols], placed[k][:, cols], ADD)
+                nc.sync.dma_start(out=out[k * P : (k + 1) * P, cols], in_=old_rows[k][:, cols])
+
+        look_up(nc.scalar, 0, 0, 1)
+        look_up(nc.vector, 0, 1, 2)
+        weigh(0, 0, 2)
+        for r in (1, 2):
+            look_up(nc.scalar, r, 0, 2)
+            weigh(r, 0, 2)
+        look_up(nc.scalar, 3, 0, 1)
+        look_up(nc.scalar, 3, 1, 2)
+        weigh(3, 0, 1)
+        weave(0)
+        round_msgs(0)
+        round_msgs(1)
+        weigh(3, 1, 2)
+        quantise_w(0)
+        quantise_m(0)
+        first = deliver_pair(0, "msgs_raw1")
+        weave(1)
+        quantise_m(1)
+        quantise_w(1)
+        place(nc.scalar, 1, first[:, 1, :], 0, HALF)
+        place(nc.vector, 0, first[:, 0, :], 0, HALF)
+        second = deliver_pair(1, "pair_sums1")
+        sums2 = deliver_whole(2)
+        sums3 = deliver_whole(3)
+        place(nc.vector, 0, second[:, 0, :], HALF, I)
+        place(nc.scalar, 1, second[:, 1, :], HALF, I)
+        place(nc.vector, 2, sums2[:, 0:SPLIT], 0, SPLIT)
+        place(nc.scalar, 3, sums3[:, 0:HALF], 0, HALF)
+        place(nc.scalar, 2, sums2[:, SPLIT:I], SPLIT, I)
+        place(nc.scalar, 3, sums3[:, HALF:I], HALF, I)
+        finish(nc.vector, 0, 1)
+        finish(nc.vector, 1, 1)
+        finish(nc.vector, 2, 1)
+        finish(nc.vector, 3, 2)

@@ -18,7 +18,9 @@ P = 128
 PACK = 4
 HALF = I // 2
 LIST_COLS = I // 16
-SPLIT = 384
+LOOKUP_V = (256, 256, 128)
+FIRST_S = 192
+SHARED_V = 384
 FLOPS = 2 * D * Q * I + 2 * Q * E * I
 
 
@@ -31,39 +33,38 @@ def tile_attend_earliertable_deliveredplanes_lean_kernel(
         sb = ctx.enter_context(tc.tile_pool(name="sb", bufs=1))
         psum = ctx.enter_context(tc.psum_pool(name="psum", bufs=1))
 
-        def slots(h):
-            return slice(h * HALF, (h + 1) * HALF)
-
         key_list = lists.tile([P, LIST_COLS], U16, name="key_list")
         earl_list = lists.tile([P, LIST_COLS], U16, name="earl_list")
         place_list = lists.tile([P, LIST_COLS], U16, name="place_list")
 
         pool_scales = sb.tile([P, T], U8, name="pool_scales", align_bytes=64)
         pool_words = sb.tile([P, T], I32, name="pool_words", align_bytes=64)
-        query_raw = sb.tile([P, PACK, Q], F32, name="query_raw")
+        query_raw = [sb.tile([P, PACK, Q // 2], F32, name=f"query_raw{u}") for u in range(2)]
         earl_rows = [sb.tile([P, Z], F32, name=f"earl_rows{r}") for r in range(PACK)]
         row_factor = sb.tile([P, PACK], F32, name="row_factor")
         msgs_raw = [sb.tile([P, PACK, 2 * P], F32, name=f"msgs_raw{u}", tag=f"msgs_raw{u}") for u in range(2)]
-        old_rows = [sb.tile([P, M], F32, name=f"old_rows{k}") for k in range(E // P)]
+        old_rows = [sb.tile([P, M], F32, name=f"old_rows{k}", tag=f"old_rows{k}") for k in range(E // P)]
         placed = [sb.tile([P, M], F32, name=f"placed{k}") for k in range(E // P)]
 
         nc.vector.memset(pool_scales[:].bitcast(I32), 0)
         for k in range(E // P):
-            nc.vector.memset(placed[k][:], 0.0)
+            (nc.vector if k < 2 else nc.gpsimd).memset(placed[k][:], 0.0)
 
         nc.sync.dma_start(key_list[:], offs)
-        nc.sync.dma_start(out=query_raw[:], in_=query.rearrange("(p j) q -> p j q", j=PACK))
+        nc.sync.dma_start(
+            out=pool_words[:], in_=keys_words[0].rearrange("p n t -> p (n t)").bitcast(I32)
+        )
         for quad in range(4):
             nc.sync.dma_start(
                 out=pool_scales[32 * quad : 32 * quad + 4, :].bitcast(I32),
                 in_=keys_scales[0, 4 * quad : 4 * quad + 4, :].bitcast(I32),
             )
-        nc.sync.dma_start(
-            out=pool_words[:], in_=keys_words[0].rearrange("p n t -> p (n t)").bitcast(I32)
-        )
+        query_by_word = query.rearrange("(p j) q -> p j q", j=PACK)
+        for u in range(2):
+            nc.sync.dma_start(out=query_raw[u][:], in_=query_by_word[:, :, u * (Q // 2) : (u + 1) * (Q // 2)])
         earl_by_place = earl.rearrange("(p r) z -> r p z", r=PACK)
-        nc.sync.dma_start(out=earl_rows[0][:], in_=earl_by_place[0])
         nc.sync.dma_start(earl_list[:], offs2)
+        nc.sync.dma_start(out=earl_rows[0][:], in_=earl_by_place[0])
         nc.sync.dma_start(out=row_factor[:], in_=qs.rearrange("(p r) o -> p (r o)", r=PACK))
         nc.sync.dma_start(place_list[:], offs3)
         for r in range(1, PACK):
@@ -74,26 +75,27 @@ def tile_attend_earliertable_deliveredplanes_lean_kernel(
         for k in range(E // P):
             nc.sync.dma_start(out=old_rows[k][:], in_=old[k * P : (k + 1) * P, :])
 
-        query_bf = sb.tile([P, PACK, P, PACK], BF16, name="query_bf", align_bytes=64)
-        nc.scalar.copy(
-            out=query_bf[:].rearrange("p r s j -> p s j r"),
-            in_=query_raw[:].rearrange("p j (s r) -> p s j r", r=PACK),
-        )
         key_scales = sb.tile([P, I], U8, name="key_scales", align_bytes=64)
         key_words = sb.tile([P, I], U32, name="key_words", align_bytes=64)
+        nc.vector.tensor_copy(key_words[:], pool_words[:].bitcast(U32).indirect(key_list[:]))
         nc.vector.tensor_copy(key_scales[:], pool_scales[:].indirect(key_list[:]))
+
+        query_bf = sb.tile([P, PACK, P, PACK], BF16, name="query_bf", align_bytes=64)
+        for u, copy in enumerate((nc.scalar.copy, nc.vector.tensor_copy)):
+            copy(
+                out=query_bf[:, :, u * (P // 2) : (u + 1) * (P // 2), :].rearrange("p r s j -> p s j r"),
+                in_=query_raw[u][:].rearrange("p j (s r) -> p s j r", r=PACK),
+            )
         query_codes = sb.tile([P, Q], U32, name="query_codes", align_bytes=64)
         query_scales = sb.tile([P, Q], U8, name="query_scales", align_bytes=64)
-        nc.vector.quantize_mx(
-            out=query_codes[:].bitcast(FP8X4),
-            scales=query_scales[:],
-            in_=query_bf[:].rearrange("p r s j -> p (r s j)"),
-        )
-        nc.vector.tensor_copy(key_words[:], pool_words[:].bitcast(U32).indirect(key_list[:]))
-
-        scores = [psum.tile([P, I], F32, name=f"scores{r}", tag=f"bank{r}") for r in range(PACK)]
+        scores = [psum.tile([P, I], F32, name=f"scores{r}") for r in range(PACK)]
         for r in range(PACK):
             cols = slice(r * P, (r + 1) * P)
+            nc.vector.quantize_mx(
+                out=query_codes[:, cols].bitcast(FP8X4),
+                scales=query_scales[:, cols],
+                in_=query_bf[:, r, :, :].rearrange("p s j -> p (s j)"),
+            )
             nc.tensor.matmul_mx(
                 out=scores[r][:],
                 lhsT=query_codes[:, cols].bitcast(FP8X4),
@@ -107,12 +109,12 @@ def tile_attend_earliertable_deliveredplanes_lean_kernel(
         earl_listed = [sb.tile([P, I], F32, name=f"earl_listed{r}") for r in range(PACK)]
         weights = sb.tile([P, 2, PACK, HALF], BF16, name="weights")
 
-        def look_up(engine, r, h0, h1):
-            window = earl_rows[r][:].indirect(earl_list[:, h0 * HALF // 16 : h1 * HALF // 16])
+        def look_up(engine, r, lo, hi):
+            window = earl_rows[r][:].indirect(earl_list[:, lo // 16 : hi // 16])
             if engine is nc.scalar:
-                nc.scalar.activation(earl_listed[r][:, h0 * HALF : h1 * HALF], window, COPY)
+                nc.scalar.activation(earl_listed[r][:, lo:hi], window, COPY)
             else:
-                nc.vector.tensor_copy(earl_listed[r][:, h0 * HALF : h1 * HALF], window)
+                nc.vector.tensor_copy(earl_listed[r][:, lo:hi], window)
 
         def weigh(r, h0, h1):
             nc.vector.scalar_tensor_tensor(
@@ -124,25 +126,26 @@ def tile_attend_earliertable_deliveredplanes_lean_kernel(
                 op1=MULT,
             )
 
-        w_bf = {}
-        w_codes = sb.tile([P, I], U32, name="w_codes", align_bytes=64)
-        w_scales = sb.tile([P, I], U8, name="w_scales", align_bytes=64)
+        w_codes = {}
+        w_scales = [sb.tile([P, HALF], U8, name=f"w_scales{h}", align_bytes=64) for h in range(2)]
 
-        def weave(h):
-            w_bf[h] = sb.tile([P, HALF, PACK], BF16, name=f"w_bf{h}", tag="w_bf", align_bytes=64)
+        def weave(h, tag):
+            woven = sb.tile([P, HALF, PACK], BF16, name=f"w_bf{h}", tag=tag, align_bytes=64)
             nc.vector.tensor_copy(
-                out=w_bf[h][:].rearrange("p (c i) r -> p c r i", i=4),
+                out=woven[:].rearrange("p (c i) r -> p c r i", i=4),
                 in_=weights[:, h, :, :].rearrange("p r (c i) -> p c r i", i=4),
             )
+            return woven
 
-        def quantise_w(h):
+        def quantise_w(h, woven, tag):
+            w_codes[h] = sb.tile([P, HALF], U32, name=f"w_codes{h}", tag=tag, align_bytes=64)
             nc.vector.quantize_mx(
-                out=w_codes[:, slots(h)].bitcast(FP8X4),
-                scales=w_scales[:, slots(h)],
-                in_=w_bf[h][:].rearrange("p i r -> p (i r)"),
+                out=w_codes[h][:].bitcast(FP8X4),
+                scales=w_scales[h][:],
+                in_=woven[:].rearrange("p i r -> p (i r)"),
             )
 
-        m_bf = [sb.tile([P, 2 * P, PACK], BF16, name=f"m_bf{u}", align_bytes=64) for u in range(2)]
+        m_bf = [sb.tile([P, 2 * P, PACK], BF16, name=f"m_bf{u}", tag=f"m_bf{u}", align_bytes=64) for u in range(2)]
         m_codes = [sb.tile([P, 2 * P], U32, name=f"m_codes{u}", align_bytes=64) for u in range(2)]
         m_scales = [sb.tile([P, 2 * P], U8, name=f"m_scales{u}", align_bytes=64) for u in range(2)]
 
@@ -159,77 +162,76 @@ def tile_attend_earliertable_deliveredplanes_lean_kernel(
                 in_=m_bf[u][:].rearrange("p e j -> p (e j)"),
             )
 
-        def product(dst, k, cols):
+        def product(dst, k, h):
             mcols = slice((k % 2) * P, (k % 2 + 1) * P)
             nc.tensor.matmul_mx(
                 out=dst,
                 lhsT=m_codes[k // 2][:, mcols].bitcast(FP8X4),
                 lhsT_scale=m_scales[k // 2][:, mcols],
-                rhs=w_codes[:, cols].bitcast(FP8X4),
-                rhs_scale=w_scales[:, cols],
+                rhs=w_codes[h][:].bitcast(FP8X4),
+                rhs_scale=w_scales[h][:],
                 start=True,
                 stop=True,
             )
 
-        def deliver_pair(h, tag):
+        def deliver_pair(h, sums):
+            cols = slice(h * HALF, (h + 1) * HALF)
             bank = psum.tile([P, 2, HALF], F32, name=f"pair_bank{h}")
             for k in range(2):
-                product(bank[:, k, :], k, slots(h))
-            sums = sb.tile([P, 2, HALF], F32, name=f"pair_sums{h}", tag=tag)
-            nc.scalar.copy(out=sums[:], in_=bank[:])
-            return sums
+                product(bank[:, k, :], k, h)
+            nc.scalar.copy(out=sums[:, :, cols], in_=bank[:])
 
-        def deliver_whole(k):
+        def deliver_whole(copy, k):
             bank = psum.tile([P, I], F32, name=f"whole_bank{k}")
-            product(bank[:], k, slice(0, I))
+            for h in range(2):
+                product(bank[:, h * HALF : (h + 1) * HALF], k, h)
             sums = sb.tile([P, I], F32, name=f"whole_sums{k}")
-            nc.scalar.copy(out=sums[:], in_=bank[:])
+            copy(out=sums[:], in_=bank[:])
             return sums
 
         def place(engine, k, values, lo, hi):
             window = placed[k][:].indirect(place_list[:, lo // 16 : hi // 16])
             if engine is nc.scalar:
-                nc.scalar.activation(window, values, COPY)
+                nc.scalar.activation(window, values[:, lo:hi], COPY)
             else:
-                nc.vector.tensor_copy(window, values)
+                nc.vector.tensor_copy(window, values[:, lo:hi])
 
-        def finish(engine, k, parts):
-            for c in range(parts):
-                cols = slice(c * (M // parts), (c + 1) * (M // parts))
-                engine.tensor_tensor(old_rows[k][:, cols], old_rows[k][:, cols], placed[k][:, cols], ADD)
-                nc.sync.dma_start(out=out[k * P : (k + 1) * P, cols], in_=old_rows[k][:, cols])
+        def finish(engine, k, cuts, tag):
+            total = sb.tile([P, M], F32, name=f"total{k}", tag=tag)
+            for lo, hi in zip(cuts, cuts[1:]):
+                engine.tensor_tensor(total[:, lo:hi], old_rows[k][:, lo:hi], placed[k][:, lo:hi], ADD)
+                nc.sync.dma_start(out=out[k * P : (k + 1) * P, lo:hi], in_=total[:, lo:hi])
 
-        look_up(nc.scalar, 0, 0, 1)
-        look_up(nc.vector, 0, 1, 2)
-        weigh(0, 0, 2)
-        for r in (1, 2):
-            look_up(nc.scalar, r, 0, 2)
+        for r in range(PACK - 1):
+            look_up(nc.vector, r, 0, LOOKUP_V[r])
+            look_up(nc.scalar, r, LOOKUP_V[r], I)
             weigh(r, 0, 2)
-        look_up(nc.scalar, 3, 0, 1)
-        look_up(nc.scalar, 3, 1, 2)
+        look_up(nc.scalar, 3, 0, HALF)
+        look_up(nc.scalar, 3, HALF, I)
         weigh(3, 0, 1)
-        weave(0)
+        woven = weave(0, "w_bf")
         round_msgs(0)
         round_msgs(1)
         weigh(3, 1, 2)
-        quantise_w(0)
+        quantise_w(0, woven, "w_codes0")
         quantise_m(0)
-        first = deliver_pair(0, "msgs_raw1")
-        weave(1)
+        pair_sums = sb.tile([P, 2, I], F32, name="pair_sums", tag="msgs_raw1")
+        deliver_pair(0, pair_sums)
+        woven = weave(1, "m_bf0")
         quantise_m(1)
-        quantise_w(1)
-        place(nc.scalar, 1, first[:, 1, :], 0, HALF)
-        place(nc.vector, 0, first[:, 0, :], 0, HALF)
-        second = deliver_pair(1, "pair_sums1")
-        sums2 = deliver_whole(2)
-        sums3 = deliver_whole(3)
-        place(nc.vector, 0, second[:, 0, :], HALF, I)
-        place(nc.scalar, 1, second[:, 1, :], HALF, I)
-        place(nc.vector, 2, sums2[:, 0:SPLIT], 0, SPLIT)
-        place(nc.scalar, 3, sums3[:, 0:HALF], 0, HALF)
-        place(nc.scalar, 2, sums2[:, SPLIT:I], SPLIT, I)
-        place(nc.scalar, 3, sums3[:, HALF:I], HALF, I)
-        finish(nc.vector, 0, 1)
-        finish(nc.vector, 1, 1)
-        finish(nc.vector, 2, 1)
-        finish(nc.vector, 3, 2)
+        quantise_w(1, woven, "m_bf1")
+        place(nc.scalar, 0, pair_sums[:, 0, :], 0, FIRST_S)
+        place(nc.vector, 1, pair_sums[:, 1, :], 0, HALF)
+        deliver_pair(1, pair_sums)
+        sums3 = deliver_whole(nc.scalar.copy, 3)
+        sums2 = deliver_whole(nc.vector.tensor_copy, 2)
+        place(nc.vector, 1, pair_sums[:, 1, :], HALF, I)
+        place(nc.vector, 2, sums2, 0, SHARED_V)
+        place(nc.scalar, 0, pair_sums[:, 0, :], FIRST_S, I)
+        place(nc.scalar, 3, sums3, 0, HALF)
+        place(nc.scalar, 2, sums2, SHARED_V, I)
+        place(nc.scalar, 3, sums3, HALF, I)
+        finish(nc.gpsimd, 1, (0, M // 2, M), "total")
+        finish(nc.vector, 0, (0, M), "old_rows1")
+        finish(nc.vector, 2, (0, M // 2, M), "old_rows0")
+        finish(nc.vector, 3, (0, M // 2, 3 * M // 4, M), "old_rows2")

@@ -18,8 +18,9 @@ P = 128
 PACK = 4
 HALF = I // 2
 LIST_COLS = I // 16
-LOOKUP_V = (256, 256, 128)
-FIRST_S = 192
+LOOKUP_V = (0, 256, 128)
+FIRST_S = 128
+QUERY_S = 52
 SHARED_V = 384
 FLOPS = 2 * D * Q * I + 2 * Q * E * I
 
@@ -39,12 +40,12 @@ def tile_attend_earliertable_deliveredplanes_lean_kernel(
 
         pool_scales = sb.tile([P, T], U8, name="pool_scales", align_bytes=64)
         pool_words = sb.tile([P, T], I32, name="pool_words", align_bytes=64)
-        query_raw = [sb.tile([P, PACK, Q // 2], F32, name=f"query_raw{u}") for u in range(2)]
+        query_raw = sb.tile([P, PACK, Q], F32, name="query_raw")
         earl_rows = [sb.tile([P, Z], F32, name=f"earl_rows{r}") for r in range(PACK)]
         row_factor = sb.tile([P, PACK], F32, name="row_factor")
         msgs_raw = [sb.tile([P, PACK, 2 * P], F32, name=f"msgs_raw{u}", tag=f"msgs_raw{u}") for u in range(2)]
         old_rows = [sb.tile([P, M], F32, name=f"old_rows{k}", tag=f"old_rows{k}") for k in range(E // P)]
-        placed = [sb.tile([P, M], F32, name=f"placed{k}") for k in range(E // P)]
+        placed = [sb.tile([P, M], F32, name=f"placed{k}", tag=f"placed{k}") for k in range(E // P)]
 
         nc.vector.memset(pool_scales[:].bitcast(I32), 0)
         for k in range(E // P):
@@ -54,20 +55,19 @@ def tile_attend_earliertable_deliveredplanes_lean_kernel(
         nc.sync.dma_start(
             out=pool_words[:], in_=keys_words[0].rearrange("p n t -> p (n t)").bitcast(I32)
         )
-        for quad in range(4):
+        for f in range(4):
             nc.sync.dma_start(
-                out=pool_scales[32 * quad : 32 * quad + 4, :].bitcast(I32),
-                in_=keys_scales[0, 4 * quad : 4 * quad + 4, :].bitcast(I32),
+                out=pool_scales[f:P:32, :].bitcast(I32),
+                in_=keys_scales[0, f:16:4, :].bitcast(I32),
             )
-        query_by_word = query.rearrange("(p j) q -> p j q", j=PACK)
-        for u in range(2):
-            nc.sync.dma_start(out=query_raw[u][:], in_=query_by_word[:, :, u * (Q // 2) : (u + 1) * (Q // 2)])
+        nc.sync.dma_start(out=query_raw[:], in_=query.rearrange("(p j) q -> p j q", j=PACK))
         earl_by_place = earl.rearrange("(p r) z -> r p z", r=PACK)
         nc.sync.dma_start(earl_list[:], offs2)
         nc.sync.dma_start(out=earl_rows[0][:], in_=earl_by_place[0])
-        nc.sync.dma_start(out=row_factor[:], in_=qs.rearrange("(p r) o -> p (r o)", r=PACK))
         nc.sync.dma_start(place_list[:], offs3)
-        for r in range(1, PACK):
+        nc.sync.dma_start(out=earl_rows[1][:], in_=earl_by_place[1])
+        nc.sync.dma_start(out=row_factor[:], in_=qs.rearrange("(p r) o -> p (r o)", r=PACK))
+        for r in range(2, PACK):
             nc.sync.dma_start(out=earl_rows[r][:], in_=earl_by_place[r])
         msgs_by_word = msgs.rearrange("(p j) e -> p j e", j=PACK)
         for u in range(2):
@@ -81,21 +81,21 @@ def tile_attend_earliertable_deliveredplanes_lean_kernel(
         nc.vector.tensor_copy(key_scales[:], pool_scales[:].indirect(key_list[:]))
 
         query_bf = sb.tile([P, PACK, P, PACK], BF16, name="query_bf", align_bytes=64)
-        for u, copy in enumerate((nc.scalar.copy, nc.vector.tensor_copy)):
+        for copy, lo, hi in ((nc.scalar.copy, 0, QUERY_S), (nc.vector.tensor_copy, QUERY_S, P)):
             copy(
-                out=query_bf[:, :, u * (P // 2) : (u + 1) * (P // 2), :].rearrange("p r s j -> p s j r"),
-                in_=query_raw[u][:].rearrange("p j (s r) -> p s j r", r=PACK),
+                out=query_bf[:, :, lo:hi, :].rearrange("p r s j -> p s j r"),
+                in_=query_raw[:, :, PACK * lo : PACK * hi].rearrange("p j (s r) -> p s j r", r=PACK),
             )
         query_codes = sb.tile([P, Q], U32, name="query_codes", align_bytes=64)
         query_scales = sb.tile([P, Q], U8, name="query_scales", align_bytes=64)
         scores = [psum.tile([P, I], F32, name=f"scores{r}") for r in range(PACK)]
+        nc.vector.quantize_mx(
+            out=query_codes[:].bitcast(FP8X4),
+            scales=query_scales[:],
+            in_=query_bf[:].rearrange("p r s j -> p (r s j)"),
+        )
         for r in range(PACK):
             cols = slice(r * P, (r + 1) * P)
-            nc.vector.quantize_mx(
-                out=query_codes[:, cols].bitcast(FP8X4),
-                scales=query_scales[:, cols],
-                in_=query_bf[:, r, :, :].rearrange("p s j -> p (s j)"),
-            )
             nc.tensor.matmul_mx(
                 out=scores[r][:],
                 lhsT=query_codes[:, cols].bitcast(FP8X4),
@@ -203,7 +203,8 @@ def tile_attend_earliertable_deliveredplanes_lean_kernel(
                 nc.sync.dma_start(out=out[k * P : (k + 1) * P, lo:hi], in_=total[:, lo:hi])
 
         for r in range(PACK - 1):
-            look_up(nc.vector, r, 0, LOOKUP_V[r])
+            if LOOKUP_V[r]:
+                look_up(nc.vector, r, 0, LOOKUP_V[r])
             look_up(nc.scalar, r, LOOKUP_V[r], I)
             weigh(r, 0, 2)
         look_up(nc.scalar, 3, 0, HALF)
@@ -223,8 +224,8 @@ def tile_attend_earliertable_deliveredplanes_lean_kernel(
         place(nc.scalar, 0, pair_sums[:, 0, :], 0, FIRST_S)
         place(nc.vector, 1, pair_sums[:, 1, :], 0, HALF)
         deliver_pair(1, pair_sums)
+        sums2 = deliver_whole(nc.scalar.copy, 2)
         sums3 = deliver_whole(nc.scalar.copy, 3)
-        sums2 = deliver_whole(nc.vector.tensor_copy, 2)
         place(nc.vector, 1, pair_sums[:, 1, :], HALF, I)
         place(nc.vector, 2, sums2, 0, SHARED_V)
         place(nc.scalar, 0, pair_sums[:, 0, :], FIRST_S, I)
@@ -232,6 +233,6 @@ def tile_attend_earliertable_deliveredplanes_lean_kernel(
         place(nc.scalar, 2, sums2, SHARED_V, I)
         place(nc.scalar, 3, sums3, HALF, I)
         finish(nc.gpsimd, 1, (0, M // 2, M), "total")
-        finish(nc.vector, 0, (0, M), "old_rows1")
-        finish(nc.vector, 2, (0, M // 2, M), "old_rows0")
-        finish(nc.vector, 3, (0, M // 2, 3 * M // 4, M), "old_rows2")
+        finish(nc.vector, 0, (0, M // 2, M), "old_rows1")
+        finish(nc.vector, 2, (0, M // 2, M), "placed1")
+        finish(nc.vector, 3, (0, M // 2, 3 * M // 4, M), "old_rows0")

@@ -14,15 +14,21 @@ ADD = mybir.AluOpType.add
 COPY = mybir.ActivationFunctionType.Copy
 
 D, T, I, Q, E, Z, M = 512, 2048, 512, 512, 512, 1024, 1024
+FLOPS = 2 * D * Q * I + 2 * Q * E * I
+
 P = 128
 PACK = 4
 HALF = I // 2
-LIST_COLS = I // 16
-LOOKUP_V = (0, 256, 128)
-FIRST_S = 128
-QUERY_S = 52
-SHARED_V = 384
-FLOPS = 2 * D * Q * I + 2 * Q * E * I
+HALF_M = M // 2
+ROW_TILES = E // P
+PER_COLUMN = 16
+RUN = 4
+QUADRANT = 32
+
+QUERY_SCALAR = 52
+EARL_VECTOR = {1: 256, 2: 128}
+SHARED_VECTOR = 384
+FIRST_SCALAR = 128
 
 
 def tile_attend_earliertable_deliveredplanes_lean_kernel(
@@ -34,9 +40,9 @@ def tile_attend_earliertable_deliveredplanes_lean_kernel(
         sb = ctx.enter_context(tc.tile_pool(name="sb", bufs=1))
         psum = ctx.enter_context(tc.psum_pool(name="psum", bufs=1))
 
-        key_list = lists.tile([P, LIST_COLS], U16, name="key_list")
-        earl_list = lists.tile([P, LIST_COLS], U16, name="earl_list")
-        place_list = lists.tile([P, LIST_COLS], U16, name="place_list")
+        key_list = lists.tile([P, I // PER_COLUMN], U16, name="key_list")
+        earl_list = lists.tile([P, I // PER_COLUMN], U16, name="earl_list")
+        place_list = lists.tile([P, I // PER_COLUMN], U16, name="place_list")
 
         pool_scales = sb.tile([P, T], U8, name="pool_scales", align_bytes=64)
         pool_words = sb.tile([P, T], I32, name="pool_words", align_bytes=64)
@@ -44,12 +50,15 @@ def tile_attend_earliertable_deliveredplanes_lean_kernel(
         earl_rows = [sb.tile([P, Z], F32, name=f"earl_rows{r}") for r in range(PACK)]
         row_factor = sb.tile([P, PACK], F32, name="row_factor")
         msgs_raw = [sb.tile([P, PACK, 2 * P], F32, name=f"msgs_raw{u}", tag=f"msgs_raw{u}") for u in range(2)]
-        old_rows = [sb.tile([P, M], F32, name=f"old_rows{k}", tag=f"old_rows{k}") for k in range(E // P)]
-        placed = [sb.tile([P, M], F32, name=f"placed{k}", tag=f"placed{k}") for k in range(E // P)]
+        old_rows = [
+            [sb.tile([P, HALF_M], F32, name=f"old_rows{k}_{c}", tag=f"old_rows{k}_{c}") for c in range(2)]
+            for k in range(ROW_TILES)
+        ]
+        placed = [sb.tile([P, M], F32, name=f"placed{k}", tag=f"placed{k}") for k in range(ROW_TILES)]
 
         nc.vector.memset(pool_scales[:].bitcast(I32), 0)
-        for k in range(E // P):
-            (nc.vector if k < 2 else nc.gpsimd).memset(placed[k][:], 0.0)
+        for k in range(ROW_TILES):
+            nc.vector.memset(placed[k][:].bitcast(I32), 0)
 
         nc.sync.dma_start(key_list[:], offs)
         nc.sync.dma_start(
@@ -57,8 +66,8 @@ def tile_attend_earliertable_deliveredplanes_lean_kernel(
         )
         for f in range(4):
             nc.sync.dma_start(
-                out=pool_scales[f:P:32, :].bitcast(I32),
-                in_=keys_scales[0, f:16:4, :].bitcast(I32),
+                out=pool_scales[f:P:QUADRANT, :].bitcast(I32),
+                in_=keys_scales[0, f : D // 32 : 4, :].bitcast(I32),
             )
         nc.sync.dma_start(out=query_raw[:], in_=query.rearrange("(p j) q -> p j q", j=PACK))
         earl_by_place = earl.rearrange("(p r) z -> r p z", r=PACK)
@@ -72,8 +81,11 @@ def tile_attend_earliertable_deliveredplanes_lean_kernel(
         msgs_by_word = msgs.rearrange("(p j) e -> p j e", j=PACK)
         for u in range(2):
             nc.sync.dma_start(out=msgs_raw[u][:], in_=msgs_by_word[:, :, u * 2 * P : (u + 1) * 2 * P])
-        for k in range(E // P):
-            nc.sync.dma_start(out=old_rows[k][:], in_=old[k * P : (k + 1) * P, :])
+        out_halves = [(k, c) for k in (1, 0, 2, 3) for c in range(2)]
+        for k, c in out_halves:
+            nc.sync.dma_start(
+                out=old_rows[k][c][:], in_=old[k * P : (k + 1) * P, c * HALF_M : (c + 1) * HALF_M]
+            )
 
         key_scales = sb.tile([P, I], U8, name="key_scales", align_bytes=64)
         key_words = sb.tile([P, I], U32, name="key_words", align_bytes=64)
@@ -81,7 +93,7 @@ def tile_attend_earliertable_deliveredplanes_lean_kernel(
         nc.vector.tensor_copy(key_scales[:], pool_scales[:].indirect(key_list[:]))
 
         query_bf = sb.tile([P, PACK, P, PACK], BF16, name="query_bf", align_bytes=64)
-        for copy, lo, hi in ((nc.scalar.copy, 0, QUERY_S), (nc.vector.tensor_copy, QUERY_S, P)):
+        for copy, lo, hi in ((nc.scalar.copy, 0, QUERY_SCALAR), (nc.vector.tensor_copy, QUERY_SCALAR, P)):
             copy(
                 out=query_bf[:, :, lo:hi, :].rearrange("p r s j -> p s j r"),
                 in_=query_raw[:, :, PACK * lo : PACK * hi].rearrange("p j (s r) -> p s j r", r=PACK),
@@ -110,7 +122,7 @@ def tile_attend_earliertable_deliveredplanes_lean_kernel(
         weights = sb.tile([P, 2, PACK, HALF], BF16, name="weights")
 
         def look_up(engine, r, lo, hi):
-            window = earl_rows[r][:].indirect(earl_list[:, lo // 16 : hi // 16])
+            window = earl_rows[r][:].indirect(earl_list[:, lo // PER_COLUMN : hi // PER_COLUMN])
             if engine is nc.scalar:
                 nc.scalar.activation(earl_listed[r][:, lo:hi], window, COPY)
             else:
@@ -130,14 +142,14 @@ def tile_attend_earliertable_deliveredplanes_lean_kernel(
         w_scales = [sb.tile([P, HALF], U8, name=f"w_scales{h}", align_bytes=64) for h in range(2)]
 
         def weave(h, tag):
-            woven = sb.tile([P, HALF, PACK], BF16, name=f"w_bf{h}", tag=tag, align_bytes=64)
+            woven = sb.tile([P, HALF, PACK], BF16, name=f"woven{h}", tag=tag, align_bytes=64)
             nc.vector.tensor_copy(
-                out=woven[:].rearrange("p (c i) r -> p c r i", i=4),
-                in_=weights[:, h, :, :].rearrange("p r (c i) -> p c r i", i=4),
+                out=woven[:].rearrange("p (c i) r -> p c r i", i=RUN),
+                in_=weights[:, h, :, :].rearrange("p r (c i) -> p c r i", i=RUN),
             )
             return woven
 
-        def quantise_w(h, woven, tag):
+        def quantise_weights(h, woven, tag):
             w_codes[h] = sb.tile([P, HALF], U32, name=f"w_codes{h}", tag=tag, align_bytes=64)
             nc.vector.quantize_mx(
                 out=w_codes[h][:].bitcast(FP8X4),
@@ -151,11 +163,11 @@ def tile_attend_earliertable_deliveredplanes_lean_kernel(
 
         def round_msgs(u):
             nc.scalar.copy(
-                out=m_bf[u][:].rearrange("p (c i) j -> p c j i", i=4),
-                in_=msgs_raw[u][:].rearrange("p j (c i) -> p c j i", i=4),
+                out=m_bf[u][:].rearrange("p (c i) j -> p c j i", i=RUN),
+                in_=msgs_raw[u][:].rearrange("p j (c i) -> p c j i", i=RUN),
             )
 
-        def quantise_m(u):
+        def quantise_msgs(u):
             nc.vector.quantize_mx(
                 out=m_codes[u][:].bitcast(FP8X4),
                 scales=m_scales[u][:],
@@ -163,11 +175,11 @@ def tile_attend_earliertable_deliveredplanes_lean_kernel(
             )
 
         def product(dst, k, h):
-            mcols = slice((k % 2) * P, (k % 2 + 1) * P)
+            cols = slice((k % 2) * P, (k % 2 + 1) * P)
             nc.tensor.matmul_mx(
                 out=dst,
-                lhsT=m_codes[k // 2][:, mcols].bitcast(FP8X4),
-                lhsT_scale=m_scales[k // 2][:, mcols],
+                lhsT=m_codes[k // 2][:, cols].bitcast(FP8X4),
+                lhsT_scale=m_scales[k // 2][:, cols],
                 rhs=w_codes[h][:].bitcast(FP8X4),
                 rhs_scale=w_scales[h][:],
                 start=True,
@@ -175,64 +187,73 @@ def tile_attend_earliertable_deliveredplanes_lean_kernel(
             )
 
         def deliver_pair(h, sums):
-            cols = slice(h * HALF, (h + 1) * HALF)
             bank = psum.tile([P, 2, HALF], F32, name=f"pair_bank{h}")
             for k in range(2):
                 product(bank[:, k, :], k, h)
-            nc.scalar.copy(out=sums[:, :, cols], in_=bank[:])
+            nc.scalar.copy(out=sums[:, :, h * HALF : (h + 1) * HALF], in_=bank[:])
 
-        def deliver_whole(copy, k):
+        def deliver_whole(k):
             bank = psum.tile([P, I], F32, name=f"whole_bank{k}")
             for h in range(2):
                 product(bank[:, h * HALF : (h + 1) * HALF], k, h)
             sums = sb.tile([P, I], F32, name=f"whole_sums{k}")
-            copy(out=sums[:], in_=bank[:])
+            nc.scalar.copy(out=sums[:], in_=bank[:])
             return sums
 
         def place(engine, k, values, lo, hi):
-            window = placed[k][:].indirect(place_list[:, lo // 16 : hi // 16])
+            window = placed[k][:].indirect(place_list[:, lo // PER_COLUMN : hi // PER_COLUMN])
             if engine is nc.scalar:
                 nc.scalar.activation(window, values[:, lo:hi], COPY)
             else:
                 nc.vector.tensor_copy(window, values[:, lo:hi])
 
-        def finish(engine, k, cuts, tag):
-            total = sb.tile([P, M], F32, name=f"total{k}", tag=tag)
-            for lo, hi in zip(cuts, cuts[1:]):
-                engine.tensor_tensor(total[:, lo:hi], old_rows[k][:, lo:hi], placed[k][:, lo:hi], ADD)
-                nc.sync.dma_start(out=out[k * P : (k + 1) * P, lo:hi], in_=total[:, lo:hi])
+        def finish(engine, k, c, pieces, tag):
+            total = sb.tile([P, HALF_M], F32, name=f"total{k}_{c}", tag=tag)
+            width = HALF_M // pieces
+            for lo in range(0, HALF_M, width):
+                cols = slice(c * HALF_M + lo, c * HALF_M + lo + width)
+                engine.tensor_tensor(
+                    total[:, lo : lo + width], old_rows[k][c][:, lo : lo + width], placed[k][:, cols], ADD
+                )
+                nc.sync.dma_start(out=out[k * P : (k + 1) * P, cols], in_=total[:, lo : lo + width])
 
-        for r in range(PACK - 1):
-            if LOOKUP_V[r]:
-                look_up(nc.vector, r, 0, LOOKUP_V[r])
-            look_up(nc.scalar, r, LOOKUP_V[r], I)
+        last = PACK - 1
+        for r in range(last):
+            split = EARL_VECTOR.get(r, 0)
+            if split:
+                look_up(nc.vector, r, 0, split)
+            look_up(nc.scalar, r, split, I)
             weigh(r, 0, 2)
-        look_up(nc.scalar, 3, 0, HALF)
-        look_up(nc.scalar, 3, HALF, I)
-        weigh(3, 0, 1)
-        woven = weave(0, "w_bf")
+        look_up(nc.scalar, last, 0, HALF)
+        look_up(nc.scalar, last, HALF, I)
+        weigh(last, 0, 1)
+        woven = weave(0, "woven0")
         round_msgs(0)
         round_msgs(1)
-        weigh(3, 1, 2)
-        quantise_w(0, woven, "w_codes0")
-        quantise_m(0)
+        weigh(last, 1, 2)
+        quantise_weights(0, woven, "w_codes0")
+        quantise_msgs(0)
         pair_sums = sb.tile([P, 2, I], F32, name="pair_sums", tag="msgs_raw1")
         deliver_pair(0, pair_sums)
         woven = weave(1, "m_bf0")
-        quantise_m(1)
-        quantise_w(1, woven, "m_bf1")
-        place(nc.scalar, 0, pair_sums[:, 0, :], 0, FIRST_S)
+        quantise_msgs(1)
+        quantise_weights(1, woven, "m_bf1")
+
+        place(nc.scalar, 0, pair_sums[:, 0, :], 0, FIRST_SCALAR)
         place(nc.vector, 1, pair_sums[:, 1, :], 0, HALF)
         deliver_pair(1, pair_sums)
-        sums2 = deliver_whole(nc.scalar.copy, 2)
-        sums3 = deliver_whole(nc.scalar.copy, 3)
+        sums2 = deliver_whole(2)
+        sums3 = deliver_whole(3)
         place(nc.vector, 1, pair_sums[:, 1, :], HALF, I)
-        place(nc.vector, 2, sums2, 0, SHARED_V)
-        place(nc.scalar, 0, pair_sums[:, 0, :], FIRST_S, I)
+        place(nc.vector, 2, sums2, 0, SHARED_VECTOR)
+        place(nc.scalar, 0, pair_sums[:, 0, :], FIRST_SCALAR, I)
         place(nc.scalar, 3, sums3, 0, HALF)
-        place(nc.scalar, 2, sums2, SHARED_V, I)
+        place(nc.scalar, 2, sums2, SHARED_VECTOR, I)
         place(nc.scalar, 3, sums3, HALF, I)
-        finish(nc.gpsimd, 1, (0, M // 2, M), "total")
-        finish(nc.vector, 0, (0, M // 2, M), "old_rows1")
-        finish(nc.vector, 2, (0, M // 2, M), "placed1")
-        finish(nc.vector, 3, (0, M // 2, 3 * M // 4, M), "old_rows0")
+
+        finish(nc.gpsimd, 1, 0, 1, "total")
+        finish(nc.vector, 1, 1, 1, "old_rows1_0")
+        finish(nc.vector, 0, 0, 1, "placed1")
+        for n in range(3, len(out_halves)):
+            k, c = out_halves[n]
+            finish(nc.vector, k, c, 2 if n == len(out_halves) - 1 else 1, "old_rows%d_%d" % out_halves[n - 2])

from contextlib import ExitStack

import concourse.mybir as mybir

F32 = mybir.dt.float32
BF16 = mybir.dt.bfloat16
I32 = mybir.dt.int32
U32 = mybir.dt.uint32
U16 = mybir.dt.uint16
U8 = mybir.dt.uint8
FP8X4 = mybir.dt.float8_e4m3fn_x4
MULT = mybir.AluOpType.mult
ADD = mybir.AluOpType.add
COPY = mybir.ActivationFunctionType.Copy

D, T, I, Q, E, Z, M = 512, 2048, 512, 512, 512, 1024, 1024
FLOPS = 2 * D * Q * I + 2 * Q * E * I

P = 128
PACK = 4
HALF = I // 2
HALF_M = M // 2
ROW_TILES = E // P
PER_COLUMN = 16
RUN = 4
QUADRANT = 32

QUERY_SCALAR = 52
EARL_VECTOR = {1: 256, 2: 128}
SHARED_VECTOR = 384
FIRST_SCALAR = 128


def tile_attend_earliertable_deliveredplanes_lean_kernel(
    tc, query, keys_words, keys_scales, earl, qs, msgs, old, offs, offs2, offs3, out
):
    nc = tc.nc
    with ExitStack() as ctx:
        lists = ctx.enter_context(tc.tile_pool(name="lists", bufs=1))
        sb = ctx.enter_context(tc.tile_pool(name="sb", bufs=1))
        psum = ctx.enter_context(tc.psum_pool(name="psum", bufs=1))

        key_list = lists.tile([P, I // PER_COLUMN], U16, name="key_list")
        earl_list = lists.tile([P, I // PER_COLUMN], U16, name="earl_list")
        place_list = lists.tile([P, I // PER_COLUMN], U16, name="place_list")

        pool_scales = sb.tile([P, T], U8, name="pool_scales", align_bytes=64)
        pool_words = sb.tile([P, T], I32, name="pool_words", align_bytes=64)
        query_raw = sb.tile([P, PACK, Q], F32, name="query_raw")
        earl_rows = [sb.tile([P, Z], F32, name=f"earl_rows{r}") for r in range(PACK)]
        row_factor = sb.tile([P, PACK], F32, name="row_factor")
        msgs_raw = [sb.tile([P, PACK, 2 * P], F32, name=f"msgs_raw{u}", tag=f"msgs_raw{u}") for u in range(2)]
        old_rows = [
            [sb.tile([P, HALF_M], F32, name=f"old_rows{k}_{c}", tag=f"old_rows{k}_{c}") for c in range(2)]
            for k in range(ROW_TILES)
        ]
        placed = [sb.tile([P, M], F32, name=f"placed{k}", tag=f"placed{k}") for k in range(ROW_TILES)]

        nc.vector.memset(pool_scales[:].bitcast(I32), 0)
        for k in range(ROW_TILES):
            nc.vector.memset(placed[k][:].bitcast(I32), 0)

        nc.sync.dma_start(key_list[:], offs)
        nc.sync.dma_start(
            out=pool_words[:], in_=keys_words[0].rearrange("p n t -> p (n t)").bitcast(I32)
        )
        for f in range(4):
            nc.sync.dma_start(
                out=pool_scales[f:P:QUADRANT, :].bitcast(I32),
                in_=keys_scales[0, f : D // 32 : 4, :].bitcast(I32),
            )
        nc.sync.dma_start(out=query_raw[:], in_=query.rearrange("(p j) q -> p j q", j=PACK))
        earl_by_place = earl.rearrange("(p r) z -> r p z", r=PACK)
        nc.sync.dma_start(earl_list[:], offs2)
        nc.sync.dma_start(out=earl_rows[0][:], in_=earl_by_place[0])
        nc.sync.dma_start(place_list[:], offs3)
        nc.sync.dma_start(out=earl_rows[1][:], in_=earl_by_place[1])
        nc.sync.dma_start(out=row_factor[:], in_=qs.rearrange("(p r) o -> p (r o)", r=PACK))
        for r in range(2, PACK):
            nc.sync.dma_start(out=earl_rows[r][:], in_=earl_by_place[r])
        msgs_by_word = msgs.rearrange("(p j) e -> p j e", j=PACK)
        for u in range(2):
            nc.sync.dma_start(out=msgs_raw[u][:], in_=msgs_by_word[:, :, u * 2 * P : (u + 1) * 2 * P])
        out_halves = [(k, c) for k in (1, 0, 2, 3) for c in range(2)]
        for k, c in out_halves:
            nc.sync.dma_start(
                out=old_rows[k][c][:], in_=old[k * P : (k + 1) * P, c * HALF_M : (c + 1) * HALF_M]
            )

        key_scales = sb.tile([P, I], U8, name="key_scales", align_bytes=64)
        key_words = sb.tile([P, I], U32, name="key_words", align_bytes=64)
        nc.vector.tensor_copy(key_words[:], pool_words[:].bitcast(U32).indirect(key_list[:]))
        nc.vector.tensor_copy(key_scales[:], pool_scales[:].indirect(key_list[:]))

        query_bf = sb.tile([P, PACK, P, PACK], BF16, name="query_bf", align_bytes=64)
        for copy, lo, hi in ((nc.scalar.copy, 0, QUERY_SCALAR), (nc.vector.tensor_copy, QUERY_SCALAR, P)):
            copy(
                out=query_bf[:, :, lo:hi, :].rearrange("p r s j -> p s j r"),
                in_=query_raw[:, :, PACK * lo : PACK * hi].rearrange("p j (s r) -> p s j r", r=PACK),
            )
        query_codes = sb.tile([P, Q], U32, name="query_codes", align_bytes=64)
        query_scales = sb.tile([P, Q], U8, name="query_scales", align_bytes=64)
        scores = [psum.tile([P, I], F32, name=f"scores{r}") for r in range(PACK)]
        nc.vector.quantize_mx(
            out=query_codes[:].bitcast(FP8X4),
            scales=query_scales[:],
            in_=query_bf[:].rearrange("p r s j -> p (r s j)"),
        )
        for r in range(PACK):
            cols = slice(r * P, (r + 1) * P)
            nc.tensor.matmul_mx(
                out=scores[r][:],
                lhsT=query_codes[:, cols].bitcast(FP8X4),
                lhsT_scale=query_scales[:, cols],
                rhs=key_words[:].bitcast(FP8X4),
                rhs_scale=key_scales[:],
                start=True,
                stop=True,
            )

        earl_listed = [sb.tile([P, I], F32, name=f"earl_listed{r}") for r in range(PACK)]
        weights = sb.tile([P, 2, PACK, HALF], BF16, name="weights")

        def look_up(engine, r, lo, hi):
            window = earl_rows[r][:].indirect(earl_list[:, lo // PER_COLUMN : hi // PER_COLUMN])
            if engine is nc.scalar:
                nc.scalar.activation(earl_listed[r][:, lo:hi], window, COPY)
            else:
                nc.vector.tensor_copy(earl_listed[r][:, lo:hi], window)

        def weigh(r, h0, h1):
            nc.vector.scalar_tensor_tensor(
                out=weights[:, h0:h1, r, :],
                in0=scores[r][:].rearrange("p (h i) -> p h i", h=2)[:, h0:h1, :],
                scalar=row_factor[:, r : r + 1],
                in1=earl_listed[r][:].rearrange("p (h i) -> p h i", h=2)[:, h0:h1, :],
                op0=MULT,
                op1=MULT,
            )

        w_codes = {}
        w_scales = [sb.tile([P, HALF], U8, name=f"w_scales{h}", align_bytes=64) for h in range(2)]

        def weave(h, tag):
            woven = sb.tile([P, HALF, PACK], BF16, name=f"woven{h}", tag=tag, align_bytes=64)
            nc.vector.tensor_copy(
                out=woven[:].rearrange("p (c i) r -> p c r i", i=RUN),
                in_=weights[:, h, :, :].rearrange("p r (c i) -> p c r i", i=RUN),
            )
            return woven

        def quantise_weights(h, woven, tag):
            w_codes[h] = sb.tile([P, HALF], U32, name=f"w_codes{h}", tag=tag, align_bytes=64)
            nc.vector.quantize_mx(
                out=w_codes[h][:].bitcast(FP8X4),
                scales=w_scales[h][:],
                in_=woven[:].rearrange("p i r -> p (i r)"),
            )

        m_bf = [sb.tile([P, 2 * P, PACK], BF16, name=f"m_bf{u}", tag=f"m_bf{u}", align_bytes=64) for u in range(2)]
        m_codes = [sb.tile([P, 2 * P], U32, name=f"m_codes{u}", align_bytes=64) for u in range(2)]
        m_scales = [sb.tile([P, 2 * P], U8, name=f"m_scales{u}", align_bytes=64) for u in range(2)]

        def round_msgs(u):
            nc.scalar.copy(
                out=m_bf[u][:].rearrange("p (c i) j -> p c j i", i=RUN),
                in_=msgs_raw[u][:].rearrange("p j (c i) -> p c j i", i=RUN),
            )

        def quantise_msgs(u):
            nc.vector.quantize_mx(
                out=m_codes[u][:].bitcast(FP8X4),
                scales=m_scales[u][:],
                in_=m_bf[u][:].rearrange("p e j -> p (e j)"),
            )

        def product(dst, k, h):
            cols = slice((k % 2) * P, (k % 2 + 1) * P)
            nc.tensor.matmul_mx(
                out=dst,
                lhsT=m_codes[k // 2][:, cols].bitcast(FP8X4),
                lhsT_scale=m_scales[k // 2][:, cols],
                rhs=w_codes[h][:].bitcast(FP8X4),
                rhs_scale=w_scales[h][:],
                start=True,
                stop=True,
            )

        def deliver_pair(h, sums):
            bank = psum.tile([P, 2, HALF], F32, name=f"pair_bank{h}")
            for k in range(2):
                product(bank[:, k, :], k, h)
            nc.scalar.copy(out=sums[:, :, h * HALF : (h + 1) * HALF], in_=bank[:])

        def deliver_whole(k):
            bank = psum.tile([P, I], F32, name=f"whole_bank{k}")
            for h in range(2):
                product(bank[:, h * HALF : (h + 1) * HALF], k, h)
            sums = sb.tile([P, I], F32, name=f"whole_sums{k}")
            nc.scalar.copy(out=sums[:], in_=bank[:])
            return sums

        def place(engine, k, values, lo, hi):
            window = placed[k][:].indirect(place_list[:, lo // PER_COLUMN : hi // PER_COLUMN])
            if engine is nc.scalar:
                nc.scalar.activation(window, values[:, lo:hi], COPY)
            else:
                nc.vector.tensor_copy(window, values[:, lo:hi])

        def finish(engine, k, c, pieces, tag):
            total = sb.tile([P, HALF_M], F32, name=f"total{k}_{c}", tag=tag)
            width = HALF_M // pieces
            for lo in range(0, HALF_M, width):
                cols = slice(c * HALF_M + lo, c * HALF_M + lo + width)
                engine.tensor_tensor(
                    total[:, lo : lo + width], old_rows[k][c][:, lo : lo + width], placed[k][:, cols], ADD
                )
                nc.sync.dma_start(out=out[k * P : (k + 1) * P, cols], in_=total[:, lo : lo + width])

        last = PACK - 1
        for r in range(last):
            split = EARL_VECTOR.get(r, 0)
            if split:
                look_up(nc.vector, r, 0, split)
            look_up(nc.scalar, r, split, I)
            weigh(r, 0, 2)
        look_up(nc.scalar, last, 0, HALF)
        look_up(nc.scalar, last, HALF, I)
        weigh(last, 0, 1)
        woven = weave(0, "woven0")
        round_msgs(0)
        round_msgs(1)
        weigh(last, 1, 2)
        quantise_weights(0, woven, "w_codes0")
        quantise_msgs(0)
        pair_sums = sb.tile([P, 2, I], F32, name="pair_sums", tag="msgs_raw1")
        deliver_pair(0, pair_sums)
        woven = weave(1, "m_bf0")
        quantise_msgs(1)
        quantise_weights(1, woven, "m_bf1")

        place(nc.scalar, 0, pair_sums[:, 0, :], 0, FIRST_SCALAR)
        place(nc.vector, 1, pair_sums[:, 1, :], 0, HALF)
        deliver_pair(1, pair_sums)
        sums2 = deliver_whole(2)
        sums3 = deliver_whole(3)
        place(nc.vector, 1, pair_sums[:, 1, :], HALF, I)
        place(nc.vector, 2, sums2, 0, SHARED_VECTOR)
        place(nc.scalar, 0, pair_sums[:, 0, :], FIRST_SCALAR, I)
        place(nc.scalar, 3, sums3, 0, HALF)
        place(nc.scalar, 2, sums2, SHARED_VECTOR, I)
        place(nc.scalar, 3, sums3, HALF, I)

        finish(nc.gpsimd, 1, 0, 1, "total")
        finish(nc.vector, 1, 1, 1, "old_rows1_0")
        finish(nc.vector, 0, 0, 1, "placed1")
        for n in range(3, len(out_halves)):
            k, c = out_halves[n]
            finish(nc.vector, k, c, 2 if n == len(out_halves) - 1 else 1, "old_rows%d_%d" % out_halves[n - 2])
